import numpy as np
import ml_dtypes


def mxq(x, axis, fmt="e4m3"):
    dtype, down = {"e4m3": (ml_dtypes.float8_e4m3fn, 7), "e5m2": (ml_dtypes.float8_e5m2, 14)}[fmt]
    v = np.moveaxis(np.asarray(x, np.float32).astype(ml_dtypes.bfloat16).astype(np.float64), axis, -1)
    blocks = v.reshape(v.shape[:-1] + (-1, 32))
    amax = np.abs(blocks).max(-1, keepdims=True)
    byte = np.maximum(np.where(amax > 0, np.frexp(amax)[1] - 1 + 127, 0) - down, 1)
    scale = np.exp2(byte - 127.0)
    codes = (blocks / scale).astype(np.float32).astype(dtype).astype(np.float64)
    return np.moveaxis((codes * scale).reshape(v.shape), -1, axis)


WIDE = False


def mx_kscale(k):
    if not WIDE:
        return np.ones(k)
    levels = np.array([10, -10, 5, -5, 0])
    if k % 512:
        return np.exp2(np.random.permutation(np.resize(levels, k // 32))).repeat(32)
    a = np.empty((k // 512, 16))
    for p in range(k // 512):
        a[p, :8] = np.random.permutation(np.resize(levels, 8))
        for g in range(8):
            far = levels[np.abs(levels - a[p, g]) >= 10]
            a[p, g + 8] = far[np.random.randint(len(far))]
    return np.exp2(a.ravel()).repeat(32)


def f64(x):
    return np.asarray(x).astype(np.float64)


def striped(idx):
    return np.tile(idx.reshape(-1, 16).T, (8, 1)).astype(np.uint16)


def unstriped(offs):
    return offs[:16].T.reshape(-1).astype(np.int64)


def pack_weight(w):
    k, n = w.shape
    w = f64(np.asarray(w, np.float32).astype(ml_dtypes.bfloat16)).reshape(k // 32, 32, n)
    amax = np.abs(w).max(1)
    byte = np.clip(np.where(amax > 0, np.frexp(amax)[1] - 1 + 127 - 7, 1), 1, 254)
    scaled = (w * np.exp2(127.0 - byte)[:, None, :]).reshape(k, n).astype(np.float32)
    words = np.ascontiguousarray(scaled.reshape(k // 512, 128, 4, n).transpose(0, 1, 3, 2)).astype(ml_dtypes.float8_e4m3fn).view(np.uint8)
    return words, np.ascontiguousarray(byte.astype(np.uint8).reshape(k // 512, 16, n))


def unpack_weight(words, scales):
    g, p, n, _ = words.shape
    vals = np.ascontiguousarray(words).view(ml_dtypes.float8_e4m3fn).astype(np.float64) * np.repeat(np.exp2(scales.astype(np.float64) - 127.0), 8, axis=1)[..., None]
    return vals.transpose(0, 1, 3, 2).reshape(g * 512, n)


K, T, S, D, N, H, V, U = 512, 2048, 1024, 4, 128, 512, 256, 512


def setup_inputs():
    n = np.random.standard_normal
    s = mx_kscale(K)[:, None]
    u = mx_kscale(H)
    packed_xT = pack_weight(n((K, T)) * s)
    return {
        "x_words": packed_xT[0],
        "x_scales": packed_xT[1],
        "hT": (n((K, H)) / np.sqrt(K) / s).astype(np.float32),
        "unit": (np.random.uniform(0.6, 1.4, (H, 1)) * u[:, None]).astype(np.float32),
        "w1": (n((H, N)) / np.sqrt(H) / u[:, None]).astype(np.float32),
        "offs": striped(np.random.permutation(T)[:S]),
        "pos": striped(np.random.permutation(np.concatenate([np.arange(V), np.random.randint(0, V, U - V)]))),
        "neg": striped(np.random.permutation(np.concatenate([np.arange(V), np.random.randint(0, V, U - V)]))),
    }


def reference(x_words, x_scales, hT, unit, w1, offs, pos, neg):
    hTq = mxq(f64(hT), 0, "e4m3")
    xq = unpack_weight(x_words, x_scales)[:, unstriped(offs)]
    y = hTq.T @ xq
    ww = np.exp(1.5 * np.tanh(y))
    wy = ww * y
    bag = (wy.reshape(len(wy), -1, D).sum(axis=2)) / (ww.reshape(len(ww), -1, D).sum(axis=2))
    bp = bag[:, unstriped(pos)]
    bn = bag[:, unstriped(neg)]
    mar = bp - bn
    ls = np.log(np.exp(-1.0 * mar) + 1.0)
    hid = f64(unit) * ls
    return mxq(f64(w1), 0, "e4m3").T @ mxq(hid, 0, "e4m3")

@@ -1,0 +1,228 @@
+from contextlib import ExitStack
+
+import concourse.mybir as mybir
+from concourse.masks import make_identity
+
+K, T, S, D, N, H, V, U = 512, 2048, 1024, 4, 128, 512, 256, 512
+
+FLOPS = 2 * K * H * S + 2 * H * N * U
+
+F32 = mybir.dt.float32
+BF16 = mybir.dt.bfloat16
+I32 = mybir.dt.int32
+U32 = mybir.dt.uint32
+U16 = mybir.dt.uint16
+U8 = mybir.dt.uint8
+FP8X4 = mybir.dt.float8_e4m3fn_x4
+ALU = mybir.AluOpType
+ACT = mybir.ActivationFunctionType
+
+P = 128
+PACK = 4
+LANES = 16
+BAG_BLOCKS = V // P
+WINDOW = 2 * U
+CLAMP = 32.0
+LEVELS = 3
+CHUNKS = 4
+R_CHUNK = U // CHUNKS
+H_FIRST = 256
+
+
+def tile_picked_ymilrk_log_p_kernel(
+    tc, x_words, x_scales, hT, unit, w1, offs, pos, neg, out
+):
+    nc = tc.nc
+    with ExitStack() as ctx:
+        keep = ctx.enter_context(tc.tile_pool(name="keep", bufs=1))
+        work = ctx.enter_context(tc.tile_pool(name="work", bufs=4))
+        psum_y = ctx.enter_context(tc.psum_pool(name="psum_y", bufs=6))
+        psum_s = ctx.enter_context(tc.psum_pool(name="psum_s", bufs=2))
+
+        offs_sb = keep.tile([P, S // LANES], U16, name="offs_sb")
+        pos_sb = keep.tile([P, U // LANES], U16, name="pos_sb")
+        neg_sb = keep.tile([P, U // LANES], U16, name="neg_sb")
+        scale_table = keep.tile([P, T], U8, name="scale_table", align_bytes=64)
+        word_table = keep.tile([P, T], U32, name="word_table", align_bytes=64)
+        h_parts = ((0, H_FIRST), (H_FIRST, H))
+        h_raw = [keep.tile([P, PACK, b - a], F32, name=f"h_raw{a}") for a, b in h_parts]
+        w_raw = keep.tile([P, PACK, N], F32, name="w_raw")
+        unit_sb = keep.tile([P, PACK], F32, name="unit_sb")
+
+        nc.vector.memset(scale_table[:].bitcast(I32), 0)
+        for q in range(4):
+            nc.scalar.dma_start(
+                out=scale_table[32 * q : 32 * q + 4, :].bitcast(I32),
+                in_=x_scales[0, 4 * q : 4 * q + 4, :].bitcast(I32),
+            )
+        nc.sync.dma_start(offs_sb[:], offs)
+        nc.sync.dma_start(
+            out=word_table[:].bitcast(I32),
+            in_=x_words[0].rearrange("p n t -> p (n t)").bitcast(I32),
+        )
+        for raw, (a, b) in zip(h_raw, h_parts):
+            nc.sync.dma_start(out=raw[:], in_=hT[:, a:b].rearrange("(p j) c -> p j c", j=PACK))
+        nc.sync.dma_start(pos_sb[:], pos)
+        nc.sync.dma_start(neg_sb[:], neg)
+        nc.sync.dma_start(out=w_raw[:], in_=w1.rearrange("(p j) n -> p j n", j=PACK))
+        nc.sync.dma_start(out=unit_sb[:], in_=unit.rearrange("(p t) o -> p (t o)", t=PACK))
+
+        ident = keep.tile([P, P], F32, name="ident")
+        make_identity(nc, ident[:])
+
+        bags = [keep.tile([P, WINDOW], F32, name=f"bag{t}") for t in range(PACK)]
+        for t in range(PACK):
+            nc.vector.memset(bags[t][:, V:], 0.0)
+
+        def pick(vb):
+            entries = offs_sb[:, vb * (P * D // LANES) : (vb + 1) * (P * D // LANES)]
+            picked = keep.tile([P, P * D], U8, name=f"picked{vb}", align_bytes=64)
+            nc.vector.tensor_copy(picked[:], scale_table[:].indirect(entries))
+            plane = keep.tile([P, D, P], U8, name=f"x_plane{vb}", align_bytes=64)
+            nc.vector.tensor_copy(out=plane[:], in_=picked[:].rearrange("p (v d) -> p d v", d=D))
+            codes = keep.tile([P, D, P], U32, name=f"x_codes{vb}", align_bytes=64)
+            nc.vector.tensor_copy(codes[:].rearrange("p d v -> p v d"), word_table[:].indirect(entries))
+            return codes, plane
+
+        h_bf = keep.tile([P, PACK, P, PACK], BF16, name="h_bf", align_bytes=64)
+        for raw, (a, b) in zip(h_raw, h_parts):
+            nc.scalar.activation(
+                out=h_bf[:, :, a // PACK : b // PACK, :].rearrange("p t m j -> p m j t"),
+                in_=raw[:].rearrange("p j (m t) -> p m j t", t=PACK),
+                func=ACT.Copy,
+            )
+
+        def quantise_h(t):
+            codes = keep.tile([P, P], U32, name=f"h_codes{t}", align_bytes=64)
+            plane = keep.tile([P, P], U8, name=f"h_plane{t}", align_bytes=64)
+            nc.vector.quantize_mx(
+                out=codes[:].bitcast(FP8X4), scales=plane[:], in_=h_bf[:, t, :, :].rearrange("p m j -> p (m j)")
+            )
+            return codes, plane
+
+        x_mx = [pick(0)]
+        h_mx = [quantise_h(t) for t in range(PACK)]
+        x_mx.append(pick(1))
+
+        w_bf = keep.tile([P, N, PACK], BF16, name="w_bf", align_bytes=64)
+        nc.scalar.activation(out=w_bf[:], in_=w_raw[:].rearrange("p j n -> p n j"), func=ACT.Copy)
+        w_codes = keep.tile([P, N], U32, name="w_codes", align_bytes=64)
+        w_plane = keep.tile([P, N], U8, name="w_plane", align_bytes=64)
+        unit_c = keep.tile([P, PACK], F32, name="unit_c")
+        nc.gpsimd.tensor_scalar(unit_c[:], unit_sb[:], 1.0 / CLAMP, 0.0, ALU.mult, ALU.add)
+
+        def weigh(t, vb):
+            y = psum_y.tile([P, D, P], F32, name="y")
+            for d in range(D):
+                nc.tensor.matmul_mx(
+                    out=y[:, d, :],
+                    lhsT=x_mx[vb][0][:, d, :].bitcast(FP8X4),
+                    lhsT_scale=x_mx[vb][1][:, d, :],
+                    rhs=h_mx[t][0][:].bitcast(FP8X4),
+                    rhs_scale=h_mx[t][1][:],
+                    start=True,
+                    stop=True,
+                )
+            th = work.tile([P, D, P], F32, name="th")
+            nc.scalar.activation(out=th[:], in_=y[:], func=ACT.Tanh)
+            ww = work.tile([P, D, P], F32, name="ww", bufs=8)
+            nc.scalar.activation(out=ww[:], in_=th[:], func=ACT.Exp, scale=1.5)
+            wy = work.tile([P, D, P], F32, name="wy", bufs=8)
+            nc.vector.tensor_tensor(wy[:], y[:], ww[:], ALU.mult)
+            return ww, wy
+
+        def add_up(sums, vb, ww, wy):
+            for half, terms in enumerate((ww, wy)):
+                for d in range(D):
+                    nc.tensor.matmul(
+                        sums[:, half, vb * P : (vb + 1) * P],
+                        terms[:, d, :],
+                        ident[:],
+                        start=(d == 0),
+                        stop=(d == D - 1),
+                        is_transpose=True,
+                    )
+
+        def divide(t, sums):
+            den = work.tile([P, V], F32, name="den")
+            nc.scalar.activation(out=den[:], in_=sums[:, 0, :], func=ACT.Copy)
+            levels = [den]
+            for lv in range(1, LEVELS + 1):
+                width = V >> lv
+                prod = work.tile([P, width], F32, name=f"prod{lv}")
+                nc.vector.tensor_tensor(prod[:], levels[-1][:, :width], levels[-1][:, width:], ALU.mult)
+                levels.append(prod)
+            smallest = work.tile([P, V >> LEVELS], F32, name="smallest")
+            nc.vector.reciprocal(smallest[:], levels[LEVELS][:])
+            inv = smallest[:]
+            for lv in reversed(range(LEVELS)):
+                width = V >> (lv + 1)
+                wider = work.tile([P, 2, width], F32, name=f"inv{lv}")
+                nc.vector.tensor_tensor(
+                    wider[:],
+                    levels[lv][:].rearrange("p (h c) -> p h c", h=2)[:, ::-1, :],
+                    inv.unsqueeze(1).to_broadcast([P, 2, width]),
+                    ALU.mult,
+                )
+                inv = wider[:].rearrange("p h c -> p (h c)")
+            nc.vector.tensor_tensor(bags[t][:, :V], sums[:, 1, :], inv, ALU.mult)
+
+        expo = keep.tile([P, PACK, U], F32, name="expo")
+        factor = keep.tile([P, PACK, U], F32, name="factor")
+        gaps = [keep.tile([P, U], F32, name=f"gap{t}") for t in range(PACK)]
+
+        def margins(t):
+            bp = work.tile([P, U], F32, name="bp")
+            nc.scalar.activation(out=bp[:], in_=bags[t][:].indirect(pos_sb[:]), func=ACT.Copy)
+            if t == 0:
+                bn = work.tile([P, U], F32, name="bn")
+                nc.scalar.activation(out=bn[:], in_=bags[t][:].indirect(neg_sb[:]), func=ACT.Copy)
+                nc.vector.tensor_tensor(gaps[t][:], bn[:], bp[:], ALU.subtract)
+            else:
+                nc.vector.tensor_tensor(gaps[t][:], bags[t][:].indirect(neg_sb[:]), bp[:], ALU.subtract)
+            low = work.tile([P, U], F32, name="low")
+            nc.vector.tensor_scalar(low[:], gaps[t][:], CLAMP, None, ALU.min)
+            nc.scalar.activation(out=expo[:, t, :], in_=low[:], func=ACT.Exp)
+
+        for t in range(PACK):
+            sums = psum_s.tile([P, 2, V], F32, name="sums")
+            for vb in range(BAG_BLOCKS):
+                add_up(sums, vb, *weigh(t, vb))
+            divide(t, sums)
+        for t in range(PACK):
+            margins(t)
+        nc.vector.quantize_mx(
+            out=w_codes[:].bitcast(FP8X4), scales=w_plane[:], in_=w_bf[:].rearrange("p n j -> p (n j)")
+        )
+        for t in range(PACK):
+            nc.vector.tensor_scalar(factor[:, t, :], gaps[t][:], CLAMP, unit_c[:, t : t + 1], ALU.max, ALU.mult)
+
+        for c in range(CHUNKS):
+            cols = slice(c * R_CHUNK, (c + 1) * R_CHUNK)
+            soft = work.tile([P, PACK, R_CHUNK], F32, name="soft")
+            nc.scalar.activation(out=soft[:], in_=expo[:, :, cols], func=ACT.Ln, bias=1.0)
+            hid = work.tile([P, R_CHUNK, PACK], BF16, name="hid", align_bytes=64)
+            nc.vector.tensor_tensor(
+                hid[:].rearrange("p (c i) t -> p c t i", i=4),
+                soft[:].rearrange("p t (c i) -> p c t i", i=4),
+                factor[:, :, cols].rearrange("p t (c i) -> p c t i", i=4),
+                ALU.mult,
+            )
+            hid_codes = work.tile([P, R_CHUNK], U32, name="hid_codes", align_bytes=64)
+            hid_plane = work.tile([P, R_CHUNK], U8, name="hid_plane", align_bytes=64)
+            nc.vector.quantize_mx(
+                out=hid_codes[:].bitcast(FP8X4), scales=hid_plane[:], in_=hid[:].rearrange("p r t -> p (r t)")
+            )
+            acc = psum_y.tile([P, R_CHUNK], F32, name="y")
+            nc.tensor.matmul_mx(
+                out=acc[:],
+                lhsT=w_codes[:].bitcast(FP8X4),
+                lhsT_scale=w_plane[:],
+                rhs=hid_codes[:].bitcast(FP8X4),
+                rhs_scale=hid_plane[:],
+                start=True,
+                stop=True,
+            )
+            res = work.tile([P, R_CHUNK], F32, name="res")
+            nc.scalar.activation(out=res[:], in_=acc[:], func=ACT.Copy)
+            nc.sync.dma_start(out=out[:, cols], in_=res[:])

@@ -23,9 +23,7 @@ LANES = 16
 BAG_BLOCKS = V // P
 WINDOW = 2 * U
 CLAMP = 32.0
-LEVELS = 3
-CHUNKS = 4
-R_CHUNK = U // CHUNKS
+EDGES = (0, 64, 192, 320, 448, 512)
 H_FIRST = 256
 
 
@@ -36,8 +34,8 @@ def tile_picked_ymilrk_log_p_kernel(
     with ExitStack() as ctx:
         keep = ctx.enter_context(tc.tile_pool(name="keep", bufs=1))
         work = ctx.enter_context(tc.tile_pool(name="work", bufs=4))
-        psum_y = ctx.enter_context(tc.psum_pool(name="psum_y", bufs=6))
-        psum_s = ctx.enter_context(tc.psum_pool(name="psum_s", bufs=2))
+        psum_y = ctx.enter_context(tc.psum_pool(name="psum_y", bufs=5))
+        psum_s = ctx.enter_context(tc.psum_pool(name="psum_s", bufs=3))
 
         offs_sb = keep.tile([P, S // LANES], U16, name="offs_sb")
         pos_sb = keep.tile([P, U // LANES], U16, name="pos_sb")
@@ -45,21 +43,21 @@ def tile_picked_ymilrk_log_p_kernel(
         scale_table = keep.tile([P, T], U8, name="scale_table", align_bytes=64)
         word_table = keep.tile([P, T], U32, name="word_table", align_bytes=64)
         h_parts = ((0, H_FIRST), (H_FIRST, H))
-        h_raw = [keep.tile([P, PACK, b - a], F32, name=f"h_raw{a}") for a, b in h_parts]
+        h_raw = [keep.tile([P, PACK, b - a], F32, name=f"h_raw{a}", tag=f"shared{a}", align_bytes=64) for a, b in h_parts]
         w_raw = keep.tile([P, PACK, N], F32, name="w_raw")
         unit_sb = keep.tile([P, PACK], F32, name="unit_sb")
 
-        nc.vector.memset(scale_table[:].bitcast(I32), 0)
+        nc.gpsimd.memset(scale_table[:].bitcast(I32), 0)
         for q in range(4):
             nc.scalar.dma_start(
                 out=scale_table[32 * q : 32 * q + 4, :].bitcast(I32),
                 in_=x_scales[0, 4 * q : 4 * q + 4, :].bitcast(I32),
             )
-        nc.sync.dma_start(offs_sb[:], offs)
         nc.sync.dma_start(
             out=word_table[:].bitcast(I32),
             in_=x_words[0].rearrange("p n t -> p (n t)").bitcast(I32),
         )
+        nc.sync.dma_start(offs_sb[:], offs)
         for raw, (a, b) in zip(h_raw, h_parts):
             nc.sync.dma_start(out=raw[:], in_=hT[:, a:b].rearrange("(p j) c -> p j c", j=PACK))
         nc.sync.dma_start(pos_sb[:], pos)
@@ -80,7 +78,7 @@ def tile_picked_ymilrk_log_p_kernel(
             nc.vector.tensor_copy(picked[:], scale_table[:].indirect(entries))
             plane = keep.tile([P, D, P], U8, name=f"x_plane{vb}", align_bytes=64)
             nc.vector.tensor_copy(out=plane[:], in_=picked[:].rearrange("p (v d) -> p d v", d=D))
-            codes = keep.tile([P, D, P], U32, name=f"x_codes{vb}", align_bytes=64)
+            codes = keep.tile([P, D, P], U32, name=f"x_codes{vb}", tag=f"shared{H_FIRST}" if vb else "first", align_bytes=64)
             nc.vector.tensor_copy(codes[:].rearrange("p d v -> p v d"), word_table[:].indirect(entries))
             return codes, plane
 
@@ -144,76 +142,66 @@ def tile_picked_ymilrk_log_p_kernel(
                     )
 
         def divide(t, sums):
-            den = work.tile([P, V], F32, name="den")
-            nc.scalar.activation(out=den[:], in_=sums[:, 0, :], func=ACT.Copy)
-            levels = [den]
-            for lv in range(1, LEVELS + 1):
-                width = V >> lv
-                prod = work.tile([P, width], F32, name=f"prod{lv}")
-                nc.vector.tensor_tensor(prod[:], levels[-1][:, :width], levels[-1][:, width:], ALU.mult)
-                levels.append(prod)
-            smallest = work.tile([P, V >> LEVELS], F32, name="smallest")
-            nc.vector.reciprocal(smallest[:], levels[LEVELS][:])
-            inv = smallest[:]
-            for lv in reversed(range(LEVELS)):
-                width = V >> (lv + 1)
-                wider = work.tile([P, 2, width], F32, name=f"inv{lv}")
-                nc.vector.tensor_tensor(
-                    wider[:],
-                    levels[lv][:].rearrange("p (h c) -> p h c", h=2)[:, ::-1, :],
-                    inv.unsqueeze(1).to_broadcast([P, 2, width]),
-                    ALU.mult,
-                )
-                inv = wider[:].rearrange("p h c -> p (h c)")
-            nc.vector.tensor_tensor(bags[t][:, :V], sums[:, 1, :], inv, ALU.mult)
+            inv_den = work.tile([P, V], F32, name="inv_den")
+            nc.vector.reciprocal(inv_den[:], sums[:, 0, :])
+            nc.vector.tensor_tensor(bags[t][:, :V], sums[:, 1, :], inv_den[:], ALU.mult)
 
         expo = keep.tile([P, PACK, U], F32, name="expo")
-        factor = keep.tile([P, PACK, U], F32, name="factor")
+        low = keep.tile([P, PACK, U], F32, name="low", tag="clamped")
         gaps = [keep.tile([P, U], F32, name=f"gap{t}") for t in range(PACK)]
 
-        def margins(t):
-            bp = work.tile([P, U], F32, name="bp")
-            nc.scalar.activation(out=bp[:], in_=bags[t][:].indirect(pos_sb[:]), func=ACT.Copy)
-            if t == 0:
-                bn = work.tile([P, U], F32, name="bn")
-                nc.scalar.activation(out=bn[:], in_=bags[t][:].indirect(neg_sb[:]), func=ACT.Copy)
-                nc.vector.tensor_tensor(gaps[t][:], bn[:], bp[:], ALU.subtract)
+        def margins(t, first, last):
+            cols = slice(first, last)
+            entries = slice(first // LANES, last // LANES)
+            bp = work.tile([P, last - first], F32, name="bp")
+            nc.scalar.activation(out=bp[:], in_=bags[t][:].indirect(pos_sb[:, entries]), func=ACT.Copy)
+            if t < PACK - 1:
+                bn = work.tile([P, last - first], F32, name="bn")
+                nc.scalar.activation(out=bn[:], in_=bags[t][:].indirect(neg_sb[:, entries]), func=ACT.Copy)
+                nc.vector.tensor_tensor(gaps[t][:, cols], bn[:], bp[:], ALU.subtract)
             else:
-                nc.vector.tensor_tensor(gaps[t][:], bags[t][:].indirect(neg_sb[:]), bp[:], ALU.subtract)
-            low = work.tile([P, U], F32, name="low")
-            nc.vector.tensor_scalar(low[:], gaps[t][:], CLAMP, None, ALU.min)
-            nc.scalar.activation(out=expo[:, t, :], in_=low[:], func=ACT.Exp)
+                nc.vector.tensor_tensor(gaps[t][:, cols], bags[t][:].indirect(neg_sb[:, entries]), bp[:], ALU.subtract)
+            nc.vector.tensor_scalar(low[:, t, cols], gaps[t][:, cols], CLAMP, None, ALU.min)
+            nc.scalar.activation(out=expo[:, t, cols], in_=low[:, t, cols], func=ACT.Exp)
 
+        sums = []
         for t in range(PACK):
-            sums = psum_s.tile([P, 2, V], F32, name="sums")
+            sums.append(psum_s.tile([P, 2, V], F32, name="sums"))
             for vb in range(BAG_BLOCKS):
-                add_up(sums, vb, *weigh(t, vb))
-            divide(t, sums)
-        for t in range(PACK):
-            margins(t)
+                add_up(sums[t], vb, *weigh(t, vb))
+            if t > 0:
+                divide(t - 1, sums[t - 1])
+        divide(PACK - 1, sums[PACK - 1])
+        margins(0, 0, U)
+        margins(1, 0, U)
+        margins(2, 0, U)
+        margins(3, 0, U // 2)
+        margins(3, U // 2, U)
         nc.vector.quantize_mx(
             out=w_codes[:].bitcast(FP8X4), scales=w_plane[:], in_=w_bf[:].rearrange("p n j -> p (n j)")
         )
+        factor = keep.tile([P, PACK, U], F32, name="factor", tag="clamped")
         for t in range(PACK):
             nc.vector.tensor_scalar(factor[:, t, :], gaps[t][:], CLAMP, unit_c[:, t : t + 1], ALU.max, ALU.mult)
 
-        for c in range(CHUNKS):
-            cols = slice(c * R_CHUNK, (c + 1) * R_CHUNK)
-            soft = work.tile([P, PACK, R_CHUNK], F32, name="soft")
+        for first, last in zip(EDGES, EDGES[1:]):
+            cols = slice(first, last)
+            width = last - first
+            soft = work.tile([P, PACK, width], F32, name="soft")
             nc.scalar.activation(out=soft[:], in_=expo[:, :, cols], func=ACT.Ln, bias=1.0)
-            hid = work.tile([P, R_CHUNK, PACK], BF16, name="hid", align_bytes=64)
+            hid = work.tile([P, width, PACK], BF16, name="hid", align_bytes=64)
             nc.vector.tensor_tensor(
                 hid[:].rearrange("p (c i) t -> p c t i", i=4),
                 soft[:].rearrange("p t (c i) -> p c t i", i=4),
                 factor[:, :, cols].rearrange("p t (c i) -> p c t i", i=4),
                 ALU.mult,
             )
-            hid_codes = work.tile([P, R_CHUNK], U32, name="hid_codes", align_bytes=64)
-            hid_plane = work.tile([P, R_CHUNK], U8, name="hid_plane", align_bytes=64)
+            hid_codes = work.tile([P, width], U32, name="hid_codes", align_bytes=64)
+            hid_plane = work.tile([P, width], U8, name="hid_plane", align_bytes=64)
             nc.vector.quantize_mx(
                 out=hid_codes[:].bitcast(FP8X4), scales=hid_plane[:], in_=hid[:].rearrange("p r t -> p (r t)")
             )
-            acc = psum_y.tile([P, R_CHUNK], F32, name="y")
+            acc = psum_y.tile([P, width], F32, name="y")
             nc.tensor.matmul_mx(
                 out=acc[:],
                 lhsT=w_codes[:].bitcast(FP8X4),
@@ -223,6 +211,6 @@ def tile_picked_ymilrk_log_p_kernel(
                 start=True,
                 stop=True,
             )
-            res = work.tile([P, R_CHUNK], F32, name="res")
+            res = work.tile([P, width], F32, name="res")
             nc.scalar.activation(out=res[:], in_=acc[:], func=ACT.Copy)
             nc.sync.dma_start(out=out[:, cols], in_=res[:])

@@ -48,15 +48,16 @@ def tile_picked_ymilrk_log_p_kernel(
         unit_sb = keep.tile([P, PACK], F32, name="unit_sb")
 
         nc.gpsimd.memset(scale_table[:].bitcast(I32), 0)
-        for q in range(4):
-            nc.scalar.dma_start(
-                out=scale_table[32 * q : 32 * q + 4, :].bitcast(I32),
-                in_=x_scales[0, 4 * q : 4 * q + 4, :].bitcast(I32),
-            )
         nc.sync.dma_start(
             out=word_table[:].bitcast(I32),
             in_=x_words[0].rearrange("p n t -> p (n t)").bitcast(I32),
         )
+        for q in range(4):
+            queue = nc.scalar if q < 2 else nc.sync
+            queue.dma_start(
+                out=scale_table[32 * q : 32 * q + 4, :].bitcast(I32),
+                in_=x_scales[0, 4 * q : 4 * q + 4, :].bitcast(I32),
+            )
         nc.sync.dma_start(offs_sb[:], offs)
         for raw, (a, b) in zip(h_raw, h_parts):
             nc.sync.dma_start(out=raw[:], in_=hT[:, a:b].rearrange("(p j) c -> p j c", j=PACK))
@@ -74,11 +75,11 @@ def tile_picked_ymilrk_log_p_kernel(
 
         def pick(vb):
             entries = offs_sb[:, vb * (P * D // LANES) : (vb + 1) * (P * D // LANES)]
-            picked = keep.tile([P, P * D], U8, name=f"picked{vb}", align_bytes=64)
+            picked = keep.tile([P, P * D], U8, name=f"picked{vb}", tag=f"shared{H_FIRST}" if vb else "first", align_bytes=64)
             nc.vector.tensor_copy(picked[:], scale_table[:].indirect(entries))
             plane = keep.tile([P, D, P], U8, name=f"x_plane{vb}", align_bytes=64)
             nc.vector.tensor_copy(out=plane[:], in_=picked[:].rearrange("p (v d) -> p d v", d=D))
-            codes = keep.tile([P, D, P], U32, name=f"x_codes{vb}", tag=f"shared{H_FIRST}" if vb else "first", align_bytes=64)
+            codes = keep.tile([P, D, P], U32, name=f"x_codes{vb}", align_bytes=64)
             nc.vector.tensor_copy(codes[:].rearrange("p d v -> p v d"), word_table[:].indirect(entries))
             return codes, plane
 
@@ -102,8 +103,6 @@ def tile_picked_ymilrk_log_p_kernel(
         h_mx = [quantise_h(t) for t in range(PACK)]
         x_mx.append(pick(1))
 
-        w_bf = keep.tile([P, N, PACK], BF16, name="w_bf", align_bytes=64)
-        nc.scalar.activation(out=w_bf[:], in_=w_raw[:].rearrange("p j n -> p n j"), func=ACT.Copy)
         w_codes = keep.tile([P, N], U32, name="w_codes", align_bytes=64)
         w_plane = keep.tile([P, N], U8, name="w_plane", align_bytes=64)
         unit_c = keep.tile([P, PACK], F32, name="unit_c")
@@ -121,7 +120,12 @@ def tile_picked_ymilrk_log_p_kernel(
                     start=True,
                     stop=True,
                 )
-            th = work.tile([P, D, P], F32, name="th")
+            if (t, vb) == (PACK - 1, BAG_BLOCKS - 1):
+                th = keep.tile([P, D, P], F32, name="th_last", tag="fetched")
+            elif (t, vb) == (1, BAG_BLOCKS - 1):
+                th = keep.tile([P, D, P], F32, name="th_mid", tag="w_bf", align_bytes=64)
+            else:
+                th = work.tile([P, D, P], F32, name="th")
             nc.scalar.activation(out=th[:], in_=y[:], func=ACT.Tanh)
             ww = work.tile([P, D, P], F32, name="ww", bufs=8)
             nc.scalar.activation(out=ww[:], in_=th[:], func=ACT.Exp, scale=1.5)
@@ -129,60 +133,69 @@ def tile_picked_ymilrk_log_p_kernel(
             nc.vector.tensor_tensor(wy[:], y[:], ww[:], ALU.mult)
             return ww, wy
 
-        def add_up(sums, vb, ww, wy):
+        def add_up(ww, wy):
+            sums = psum_s.tile([P, 2, P], F32, name="sums")
             for half, terms in enumerate((ww, wy)):
                 for d in range(D):
                     nc.tensor.matmul(
-                        sums[:, half, vb * P : (vb + 1) * P],
-                        terms[:, d, :],
-                        ident[:],
-                        start=(d == 0),
-                        stop=(d == D - 1),
-                        is_transpose=True,
+                        sums[:, half, :], terms[:, d, :], ident[:], start=(d == 0), stop=(d == D - 1), is_transpose=True
                     )
+            return sums
 
-        def divide(t, sums):
-            inv_den = work.tile([P, V], F32, name="inv_den")
+        def divide(t, vb, sums):
+            inv_den = keep.tile([P, P], F32, name="inv_den", tag=f"inv{t}{vb}")
             nc.vector.reciprocal(inv_den[:], sums[:, 0, :])
-            nc.vector.tensor_tensor(bags[t][:, :V], sums[:, 1, :], inv_den[:], ALU.mult)
+            nc.vector.tensor_tensor(bags[t][:, vb * P : (vb + 1) * P], sums[:, 1, :], inv_den[:], ALU.mult)
 
+        blocks = [(0, 0), (1, 0), (0, 1), (1, 1), (2, 0), (2, 1), (3, 0), (3, 1)]
+        terms = [weigh(t, vb) for t, vb in blocks]
+        for (t, vb), (ww, wy) in zip(blocks, terms):
+            divide(t, vb, add_up(ww, wy))
+
+        w_bf = keep.tile([P, N, PACK], BF16, name="w_bf", tag="w_bf", align_bytes=64)
+        nc.gpsimd.tensor_copy(out=w_bf[:], in_=w_raw[:].rearrange("p j n -> p n j"))
+
+        fetched = keep.tile([P, 2 * PACK - 1, U], F32, name="fetched", tag="fetched")
+        early_gap = keep.tile([P, 2, U], F32, name="early_gap")
+        late = keep.tile([P, PACK + 2, U], F32, name="late", tag="inv31")
         expo = keep.tile([P, PACK, U], F32, name="expo")
-        low = keep.tile([P, PACK, U], F32, name="low", tag="clamped")
-        gaps = [keep.tile([P, U], F32, name=f"gap{t}") for t in range(PACK)]
+        low = late[:, :PACK, :]
+        factor = late[:, :PACK, :]
+        gaps = [early_gap[:, 0, :], early_gap[:, 1, :], late[:, PACK, :], late[:, PACK + 1, :]]
+        last_t = PACK - 1
+        halves = [slice(0, U // 2), slice(U // 2, U)]
 
-        def margins(t, first, last):
-            cols = slice(first, last)
-            entries = slice(first // LANES, last // LANES)
-            bp = work.tile([P, last - first], F32, name="bp")
-            nc.scalar.activation(out=bp[:], in_=bags[t][:].indirect(pos_sb[:, entries]), func=ACT.Copy)
-            if t < PACK - 1:
-                bn = work.tile([P, last - first], F32, name="bn")
-                nc.scalar.activation(out=bn[:], in_=bags[t][:].indirect(neg_sb[:, entries]), func=ACT.Copy)
-                nc.vector.tensor_tensor(gaps[t][:, cols], bn[:], bp[:], ALU.subtract)
-            else:
-                nc.vector.tensor_tensor(gaps[t][:, cols], bags[t][:].indirect(neg_sb[:, entries]), bp[:], ALU.subtract)
-            nc.vector.tensor_scalar(low[:, t, cols], gaps[t][:, cols], CLAMP, None, ALU.min)
-            nc.scalar.activation(out=expo[:, t, cols], in_=low[:, t, cols], func=ACT.Exp)
+        def entries(lst, cols):
+            return lst[:, cols.start // LANES : cols.stop // LANES]
 
-        sums = []
-        for t in range(PACK):
-            sums.append(psum_s.tile([P, 2, V], F32, name="sums"))
-            for vb in range(BAG_BLOCKS):
-                add_up(sums[t], vb, *weigh(t, vb))
-            if t > 0:
-                divide(t - 1, sums[t - 1])
-        divide(PACK - 1, sums[PACK - 1])
-        margins(0, 0, U)
-        margins(1, 0, U)
-        margins(2, 0, U)
-        margins(3, 0, U // 2)
-        margins(3, U // 2, U)
+        for t in range(last_t):
+            nc.scalar.activation(out=fetched[:, t, :], in_=bags[t][:].indirect(pos_sb[:]), func=ACT.Copy)
+            nc.scalar.activation(out=fetched[:, PACK + t, :], in_=bags[t][:].indirect(neg_sb[:]), func=ACT.Copy)
+        for cols in halves:
+            nc.scalar.activation(
+                out=fetched[:, last_t, cols], in_=bags[last_t][:].indirect(entries(pos_sb, cols)), func=ACT.Copy
+            )
+        for t in range(2):
+            nc.gpsimd.tensor_tensor(gaps[t], fetched[:, PACK + t, :], fetched[:, t, :], ALU.subtract)
+        nc.vector.tensor_scalar(low[:, :2, :], early_gap[:], CLAMP, None, ALU.min)
+        nc.scalar.activation(out=expo[:, :2, :], in_=low[:, :2, :], func=ACT.Exp)
+        nc.vector.tensor_tensor(gaps[2], fetched[:, PACK + 2, :], fetched[:, 2, :], ALU.subtract)
+        nc.vector.tensor_scalar(low[:, 2, :], gaps[2], CLAMP, None, ALU.min)
+        nc.scalar.activation(out=expo[:, 2, :], in_=low[:, 2, :], func=ACT.Exp)
+        for cols in halves:
+            nc.vector.tensor_tensor(
+                gaps[last_t][:, cols],
+                bags[last_t][:].indirect(entries(neg_sb, cols)),
+                fetched[:, last_t, cols],
+                ALU.subtract,
+            )
+            nc.vector.tensor_scalar(low[:, last_t, cols], gaps[last_t][:, cols], CLAMP, None, ALU.min)
+            nc.scalar.activation(out=expo[:, last_t, cols], in_=low[:, last_t, cols], func=ACT.Exp)
         nc.vector.quantize_mx(
             out=w_codes[:].bitcast(FP8X4), scales=w_plane[:], in_=w_bf[:].rearrange("p n j -> p (n j)")
         )
-        factor = keep.tile([P, PACK, U], F32, name="factor", tag="clamped")
         for t in range(PACK):
-            nc.vector.tensor_scalar(factor[:, t, :], gaps[t][:], CLAMP, unit_c[:, t : t + 1], ALU.max, ALU.mult)
+            nc.vector.tensor_scalar(factor[:, t, :], gaps[t], CLAMP, unit_c[:, t : t + 1], ALU.max, ALU.mult)
 
         for first, last in zip(EDGES, EDGES[1:]):
             cols = slice(first, last)

from contextlib import ExitStack

import concourse.mybir as mybir
from concourse.masks import make_identity

K, T, S, D, N, H, V, U = 512, 2048, 1024, 4, 128, 512, 256, 512

FLOPS = 2 * K * H * S + 2 * H * N * U

F32 = mybir.dt.float32
BF16 = mybir.dt.bfloat16
I32 = mybir.dt.int32
U32 = mybir.dt.uint32
U16 = mybir.dt.uint16
U8 = mybir.dt.uint8
FP8X4 = mybir.dt.float8_e4m3fn_x4
ALU = mybir.AluOpType
ACT = mybir.ActivationFunctionType

P = 128
PACK = 4
LANES = 16
BAG_BLOCKS = V // P
WINDOW = 2 * U
CLAMP = 32.0
EDGES = (0, 64, 192, 320, 448, 512)
H_FIRST = 256


def tile_picked_ymilrk_log_p_kernel(
    tc, x_words, x_scales, hT, unit, w1, offs, pos, neg, out
):
    nc = tc.nc
    with ExitStack() as ctx:
        keep = ctx.enter_context(tc.tile_pool(name="keep", bufs=1))
        work = ctx.enter_context(tc.tile_pool(name="work", bufs=4))
        psum_y = ctx.enter_context(tc.psum_pool(name="psum_y", bufs=5))
        psum_s = ctx.enter_context(tc.psum_pool(name="psum_s", bufs=3))

        offs_sb = keep.tile([P, S // LANES], U16, name="offs_sb")
        pos_sb = keep.tile([P, U // LANES], U16, name="pos_sb")
        neg_sb = keep.tile([P, U // LANES], U16, name="neg_sb")
        scale_table = keep.tile([P, T], U8, name="scale_table", align_bytes=64)
        word_table = keep.tile([P, T], U32, name="word_table", align_bytes=64)
        h_parts = ((0, H_FIRST), (H_FIRST, H))
        h_raw = [keep.tile([P, PACK, b - a], F32, name=f"h_raw{a}", tag=f"shared{a}", align_bytes=64) for a, b in h_parts]
        w_raw = keep.tile([P, PACK, N], F32, name="w_raw")
        unit_sb = keep.tile([P, PACK], F32, name="unit_sb")

        nc.gpsimd.memset(scale_table[:].bitcast(I32), 0)
        nc.sync.dma_start(
            out=word_table[:].bitcast(I32),
            in_=x_words[0].rearrange("p n t -> p (n t)").bitcast(I32),
        )
        for q in range(4):
            queue = nc.scalar if q < 2 else nc.sync
            queue.dma_start(
                out=scale_table[32 * q : 32 * q + 4, :].bitcast(I32),
                in_=x_scales[0, 4 * q : 4 * q + 4, :].bitcast(I32),
            )
        nc.sync.dma_start(offs_sb[:], offs)
        for raw, (a, b) in zip(h_raw, h_parts):
            nc.sync.dma_start(out=raw[:], in_=hT[:, a:b].rearrange("(p j) c -> p j c", j=PACK))
        nc.sync.dma_start(pos_sb[:], pos)
        nc.sync.dma_start(neg_sb[:], neg)
        nc.sync.dma_start(out=w_raw[:], in_=w1.rearrange("(p j) n -> p j n", j=PACK))
        nc.sync.dma_start(out=unit_sb[:], in_=unit.rearrange("(p t) o -> p (t o)", t=PACK))

        ident = keep.tile([P, P], F32, name="ident")
        make_identity(nc, ident[:])

        bags = [keep.tile([P, WINDOW], F32, name=f"bag{t}") for t in range(PACK)]
        for t in range(PACK):
            nc.vector.memset(bags[t][:, V:], 0.0)

        def pick(vb):
            entries = offs_sb[:, vb * (P * D // LANES) : (vb + 1) * (P * D // LANES)]
            picked = keep.tile([P, P * D], U8, name=f"picked{vb}", tag=f"shared{H_FIRST}" if vb else "first", align_bytes=64)
            nc.vector.tensor_copy(picked[:], scale_table[:].indirect(entries))
            plane = keep.tile([P, D, P], U8, name=f"x_plane{vb}", align_bytes=64)
            nc.vector.tensor_copy(out=plane[:], in_=picked[:].rearrange("p (v d) -> p d v", d=D))
            codes = keep.tile([P, D, P], U32, name=f"x_codes{vb}", align_bytes=64)
            nc.vector.tensor_copy(codes[:].rearrange("p d v -> p v d"), word_table[:].indirect(entries))
            return codes, plane

        h_bf = keep.tile([P, PACK, P, PACK], BF16, name="h_bf", align_bytes=64)
        for raw, (a, b) in zip(h_raw, h_parts):
            nc.scalar.activation(
                out=h_bf[:, :, a // PACK : b // PACK, :].rearrange("p t m j -> p m j t"),
                in_=raw[:].rearrange("p j (m t) -> p m j t", t=PACK),
                func=ACT.Copy,
            )

        def quantise_h(t):
            codes = keep.tile([P, P], U32, name=f"h_codes{t}", align_bytes=64)
            plane = keep.tile([P, P], U8, name=f"h_plane{t}", align_bytes=64)
            nc.vector.quantize_mx(
                out=codes[:].bitcast(FP8X4), scales=plane[:], in_=h_bf[:, t, :, :].rearrange("p m j -> p (m j)")
            )
            return codes, plane

        x_mx = [pick(0)]
        h_mx = [quantise_h(t) for t in range(PACK)]
        x_mx.append(pick(1))

        w_codes = keep.tile([P, N], U32, name="w_codes", align_bytes=64)
        w_plane = keep.tile([P, N], U8, name="w_plane", align_bytes=64)
        unit_c = keep.tile([P, PACK], F32, name="unit_c")
        nc.gpsimd.tensor_scalar(unit_c[:], unit_sb[:], 1.0 / CLAMP, 0.0, ALU.mult, ALU.add)

        def weigh(t, vb):
            y = psum_y.tile([P, D, P], F32, name="y")
            for d in range(D):
                nc.tensor.matmul_mx(
                    out=y[:, d, :],
                    lhsT=x_mx[vb][0][:, d, :].bitcast(FP8X4),
                    lhsT_scale=x_mx[vb][1][:, d, :],
                    rhs=h_mx[t][0][:].bitcast(FP8X4),
                    rhs_scale=h_mx[t][1][:],
                    start=True,
                    stop=True,
                )
            if (t, vb) == (PACK - 1, BAG_BLOCKS - 1):
                th = keep.tile([P, D, P], F32, name="th_last", tag="fetched")
            elif (t, vb) == (1, BAG_BLOCKS - 1):
                th = keep.tile([P, D, P], F32, name="th_mid", tag="w_bf", align_bytes=64)
            else:
                th = work.tile([P, D, P], F32, name="th")
            nc.scalar.activation(out=th[:], in_=y[:], func=ACT.Tanh)
            ww = work.tile([P, D, P], F32, name="ww", bufs=8)
            nc.scalar.activation(out=ww[:], in_=th[:], func=ACT.Exp, scale=1.5)
            wy = work.tile([P, D, P], F32, name="wy", bufs=8)
            nc.vector.tensor_tensor(wy[:], y[:], ww[:], ALU.mult)
            return ww, wy

        def add_up(ww, wy):
            sums = psum_s.tile([P, 2, P], F32, name="sums")
            for half, terms in enumerate((ww, wy)):
                for d in range(D):
                    nc.tensor.matmul(
                        sums[:, half, :], terms[:, d, :], ident[:], start=(d == 0), stop=(d == D - 1), is_transpose=True
                    )
            return sums

        def divide(t, vb, sums):
            inv_den = keep.tile([P, P], F32, name="inv_den", tag=f"inv{t}{vb}")
            nc.vector.reciprocal(inv_den[:], sums[:, 0, :])
            nc.vector.tensor_tensor(bags[t][:, vb * P : (vb + 1) * P], sums[:, 1, :], inv_den[:], ALU.mult)

        blocks = [(0, 0), (1, 0), (0, 1), (1, 1), (2, 0), (2, 1), (3, 0), (3, 1)]
        terms = [weigh(t, vb) for t, vb in blocks]
        for (t, vb), (ww, wy) in zip(blocks, terms):
            divide(t, vb, add_up(ww, wy))

        w_bf = keep.tile([P, N, PACK], BF16, name="w_bf", tag="w_bf", align_bytes=64)
        nc.gpsimd.tensor_copy(out=w_bf[:], in_=w_raw[:].rearrange("p j n -> p n j"))

        fetched = keep.tile([P, 2 * PACK - 1, U], F32, name="fetched", tag="fetched")
        early_gap = keep.tile([P, 2, U], F32, name="early_gap")
        late = keep.tile([P, PACK + 2, U], F32, name="late", tag="inv31")
        expo = keep.tile([P, PACK, U], F32, name="expo")
        low = late[:, :PACK, :]
        factor = late[:, :PACK, :]
        gaps = [early_gap[:, 0, :], early_gap[:, 1, :], late[:, PACK, :], late[:, PACK + 1, :]]
        last_t = PACK - 1
        halves = [slice(0, U // 2), slice(U // 2, U)]

        def entries(lst, cols):
            return lst[:, cols.start // LANES : cols.stop // LANES]

        for t in range(last_t):
            nc.scalar.activation(out=fetched[:, t, :], in_=bags[t][:].indirect(pos_sb[:]), func=ACT.Copy)
            nc.scalar.activation(out=fetched[:, PACK + t, :], in_=bags[t][:].indirect(neg_sb[:]), func=ACT.Copy)
        for cols in halves:
            nc.scalar.activation(
                out=fetched[:, last_t, cols], in_=bags[last_t][:].indirect(entries(pos_sb, cols)), func=ACT.Copy
            )
        for t in range(2):
            nc.gpsimd.tensor_tensor(gaps[t], fetched[:, PACK + t, :], fetched[:, t, :], ALU.subtract)
        nc.vector.tensor_scalar(low[:, :2, :], early_gap[:], CLAMP, None, ALU.min)
        nc.scalar.activation(out=expo[:, :2, :], in_=low[:, :2, :], func=ACT.Exp)
        nc.vector.tensor_tensor(gaps[2], fetched[:, PACK + 2, :], fetched[:, 2, :], ALU.subtract)
        nc.vector.tensor_scalar(low[:, 2, :], gaps[2], CLAMP, None, ALU.min)
        nc.scalar.activation(out=expo[:, 2, :], in_=low[:, 2, :], func=ACT.Exp)
        for cols in halves:
            nc.vector.tensor_tensor(
                gaps[last_t][:, cols],
                bags[last_t][:].indirect(entries(neg_sb, cols)),
                fetched[:, last_t, cols],
                ALU.subtract,
            )
            nc.vector.tensor_scalar(low[:, last_t, cols], gaps[last_t][:, cols], CLAMP, None, ALU.min)
            nc.scalar.activation(out=expo[:, last_t, cols], in_=low[:, last_t, cols], func=ACT.Exp)
        nc.vector.quantize_mx(
            out=w_codes[:].bitcast(FP8X4), scales=w_plane[:], in_=w_bf[:].rearrange("p n j -> p (n j)")
        )
        for t in range(PACK):
            nc.vector.tensor_scalar(factor[:, t, :], gaps[t], CLAMP, unit_c[:, t : t + 1], ALU.max, ALU.mult)

        for first, last in zip(EDGES, EDGES[1:]):
            cols = slice(first, last)
            width = last - first
            soft = work.tile([P, PACK, width], F32, name="soft")
            nc.scalar.activation(out=soft[:], in_=expo[:, :, cols], func=ACT.Ln, bias=1.0)
            hid = work.tile([P, width, PACK], BF16, name="hid", align_bytes=64)
            nc.vector.tensor_tensor(
                hid[:].rearrange("p (c i) t -> p c t i", i=4),
                soft[:].rearrange("p t (c i) -> p c t i", i=4),
                factor[:, :, cols].rearrange("p t (c i) -> p c t i", i=4),
                ALU.mult,
            )
            hid_codes = work.tile([P, width], U32, name="hid_codes", align_bytes=64)
            hid_plane = work.tile([P, width], U8, name="hid_plane", align_bytes=64)
            nc.vector.quantize_mx(
                out=hid_codes[:].bitcast(FP8X4), scales=hid_plane[:], in_=hid[:].rearrange("p r t -> p (r t)")
            )
            acc = psum_y.tile([P, width], F32, name="y")
            nc.tensor.matmul_mx(
                out=acc[:],
                lhsT=w_codes[:].bitcast(FP8X4),
                lhsT_scale=w_plane[:],
                rhs=hid_codes[:].bitcast(FP8X4),
                rhs_scale=hid_plane[:],
                start=True,
                stop=True,
            )
            res = work.tile([P, width], F32, name="res")
            nc.scalar.activation(out=res[:], in_=acc[:], func=ACT.Copy)
            nc.sync.dma_start(out=out[:, cols], in_=res[:])
